import numpy as np
import ml_dtypes


def mxq(x, axis, fmt="e4m3"):
    dtype, down = {"e4m3": (ml_dtypes.float8_e4m3fn, 7), "e5m2": (ml_dtypes.float8_e5m2, 14)}[fmt]
    v = np.moveaxis(np.asarray(x, np.float32).astype(ml_dtypes.bfloat16).astype(np.float64), axis, -1)
    blocks = v.reshape(v.shape[:-1] + (-1, 32))
    amax = np.abs(blocks).max(-1, keepdims=True)
    byte = np.maximum(np.where(amax > 0, np.frexp(amax)[1] - 1 + 127, 0) - down, 1)
    scale = np.exp2(byte - 127.0)
    codes = (blocks / scale).astype(np.float32).astype(dtype).astype(np.float64)
    return np.moveaxis((codes * scale).reshape(v.shape), -1, axis)


WIDE = False


def mx_kscale(k):
    if not WIDE:
        return np.ones(k)
    levels = np.array([10, -10, 5, -5, 0])
    if k % 512:
        return np.exp2(np.random.permutation(np.resize(levels, k // 32))).repeat(32)
    a = np.empty((k // 512, 16))
    for p in range(k // 512):
        a[p, :8] = np.random.permutation(np.resize(levels, 8))
        for g in range(8):
            far = levels[np.abs(levels - a[p, g]) >= 10]
            a[p, g + 8] = far[np.random.randint(len(far))]
    return np.exp2(a.ravel()).repeat(32)


def f64(x):
    return np.asarray(x).astype(np.float64)


def striped(idx):
    return np.tile(np.asarray(idx).reshape(-1, 16).T, (8, 1)).astype(np.uint16)


def unstriped(offs):
    return offs[:16].T.reshape(-1).astype(np.int64)


def striped8(idx):
    return np.asarray(idx).reshape(8, -1, 16).transpose(0, 2, 1).reshape(128, -1).astype(np.uint16)


def unstriped8(offs):
    return offs.reshape(8, 16, -1).transpose(0, 2, 1).reshape(8, -1).astype(np.int64)


def pick8(x, idx, run):
    r = np.arange(len(x))
    return x[r[:, None], idx[r % (8 * run) // run]]


E2M1 = np.array([0.0, 0.5, 1.0, 1.5, 2.0, 3.0, 4.0, 6.0, -0.0, -0.5, -1.0, -1.5, -2.0, -3.0, -4.0, -6.0])


def pack_weight(w, fmt):
    k, n = w.shape
    w = f64(np.asarray(w, np.float32).astype(ml_dtypes.bfloat16)).reshape(k // 32, 32, n)
    amax = np.abs(w).max(1)
    if fmt == "e4m3":
        byte = np.frexp(amax)[1] - 1 + 127 - 7
    else:
        mant, ex = np.frexp(amax / 6.0)
        byte = np.where(mant > 0.5, ex, ex - 1) + 127
    byte = np.clip(np.where(amax > 0, byte, 1), 1, 254)
    scaled = (w * np.exp2(127.0 - byte)[:, None, :]).reshape(k, n).astype(np.float32)
    by_word = np.ascontiguousarray(scaled.reshape(k // 512, 128, 4, n).transpose(0, 1, 3, 2))
    if fmt == "e4m3":
        words = by_word.astype(ml_dtypes.float8_e4m3fn).view(np.uint8)
    else:
        c = by_word.astype(ml_dtypes.float4_e2m1fn).view(np.uint8) & 0xF
        words = (c[..., 0::2] | (c[..., 1::2] << 4)).reshape(k // 512, 128, 2 * n)
    return np.ascontiguousarray(words), np.ascontiguousarray(byte.astype(np.uint8).reshape(k // 512, 16, n))


def unpack_weight(words, scales, fmt):
    g, _, n = scales.shape
    words = np.ascontiguousarray(words).reshape(g, 128, n, -1)
    if fmt == "e4m3":
        vals = words.view(ml_dtypes.float8_e4m3fn).astype(np.float64)
    else:
        nib = np.empty((g, 128, n, 4), np.uint8)
        nib[..., 0::2] = words & 0xF
        nib[..., 1::2] = words >> 4
        vals = E2M1[nib]
    vals = vals * np.repeat(np.exp2(scales.astype(np.float64) - 127.0), 8, axis=1)[..., None]
    return vals.transpose(0, 1, 3, 2).reshape(g * 512, n)


def sigmoid(v):
    return 1.0 / (1.0 + np.exp(-v))


def bf(x):
    return np.asarray(x, np.float32).astype(ml_dtypes.bfloat16)


def planes(Y):
    r, m = Y.shape
    b = f64(bf(Y)).reshape(r // 32, 32, m)
    amax = np.abs(b).max(1)
    byte = np.clip(np.where(amax > 0, np.frexp(amax)[1] - 1 + 127 - 7, 1), 1, 254)
    codes = (b * np.exp2(127.0 - byte)[:, None, :]).reshape(r, m).astype(np.float32).astype(ml_dtypes.float8_e4m3fn).view(np.uint8)
    words = codes.reshape(r // 512, 128, 4, m).transpose(0, 1, 3, 2)
    return np.ascontiguousarray(words), np.ascontiguousarray(byte.astype(np.uint8).reshape(r // 512, 16, m))


K, R, F, T, J, U = 512, 512, 512, 2048, 256, 512


def setup_inputs():
    n = np.random.standard_normal
    idx = np.random.permutation(T)[:J]
    idx2 = np.stack([np.random.permutation(U)[:J] for _ in range(8)])
    fk = mx_kscale(K)
    fr = mx_kscale(R)
    tabp = pack_weight(n((K, T)) / fk[:, None], "e2m1")
    return {
        "tab_words": tabp[0],
        "tab_scales": tabp[1],
        "w1": (n((K, R)) * 1 / np.sqrt(K) * fk[:, None]).astype(np.float32),
        "gain": (np.random.uniform(0.5, 1.5, (R, 1))).astype(np.float32),
        "ground": (n((R, U)) * 1.0).astype(np.float32),
        "rs": (np.random.uniform(0.5, 2.0, (R, 1)) * fr[:, None]).astype(np.float32),
        "wor": (n((R, F)) * 1 / np.sqrt(R) / fr[:, None]).astype(np.float32),
        "res": (n((F, U)) * 0.5).astype(np.float32),
        "offs": striped(idx),
        "offs2": striped8(idx2),
    }


def reference(tab_words, tab_scales, w1, gain, ground, rs, wor, res, offs, offs2):
    idx = unstriped(offs)
    idx2 = unstriped8(offs2)
    tabu = unpack_weight(tab_words, tab_scales, "e2m1")
    w1q = mxq(f64(w1), 0, "e4m3")
    tabidxg = tabu[:, idx]
    a = w1q.T @ tabidxg
    h1 = a * f64(gain)
    pg = np.zeros((R, U))
    pg[np.arange(R)[:, None], idx2[np.arange(R) % 512 // 64]] = h1
    gt = sigmoid(pg)
    u1 = pg + f64(ground) * gt
    fo1 = u1 * f64(rs)
    worq = mxq(f64(wor), 0, "e4m3")
    fo1q = mxq(fo1, 0, "e4m3")
    yo = worq.T @ fo1q
    y = yo + f64(res)
    words, scales = planes(y)
    return y, words, scales

@@ -1,0 +1,193 @@
+from contextlib import ExitStack
+
+import concourse.mybir as mybir
+
+K, R, F, T, J, U = 512, 512, 512, 2048, 256, 512
+FLOPS = 2 * K * R * J + 2 * R * F * U
+
+F32 = mybir.dt.float32
+BF16 = mybir.dt.bfloat16
+I32 = mybir.dt.int32
+U32 = mybir.dt.uint32
+U16 = mybir.dt.uint16
+U8 = mybir.dt.uint8
+FP8X4 = mybir.dt.float8_e4m3fn_x4
+FP4X4 = mybir.dt.float4_e2m1fn_x4
+MULT = mybir.AluOpType.mult
+ADD = mybir.AluOpType.add
+COPY = mybir.ActivationFunctionType.Copy
+SIGMOID = mybir.ActivationFunctionType.Sigmoid
+
+P = 128
+PACK = 4
+HALF = P // 2
+CHUNK = 128
+CHUNKS = U // CHUNK
+W1_VECTOR_SHARE = 44
+WOR_PIECE = 32
+
+
+def deal(copy, dealt, raw, first, m0, m1):
+    copy(
+        dealt[:, :, first + m0 : first + m1, :].rearrange("p t m j -> p m j t"),
+        raw[:, :, PACK * m0 : PACK * m1].rearrange("p j (m t) -> p m j t", t=PACK),
+    )
+
+
+def pairs_out(words):
+    return words.rearrange("p (c i t) -> p c t i", i=2, t=PACK)
+
+
+def pairs_in(rows):
+    return rows.rearrange("p t (c i) -> p c t i", i=2)
+
+
+def tile_attend_chgroundgate_pl_kernel(tc, tab_words, tab_scales, w1, gain, ground, rs, wor, res, offs, offs2, out_0, out_1, out_2):
+    nc = tc.nc
+    with ExitStack() as ctx:
+        keep = ctx.enter_context(tc.tile_pool(name="keep", bufs=1))
+        psum = ctx.enter_context(tc.psum_pool(name="psum", bufs=1))
+
+        offs_sb = keep.tile([P, J // 16], U16)
+        nc.sync.dma_start(offs_sb[:], offs)
+
+        table_scales = keep.tile([P, T], U8, tag="scales_then_ground")
+        nc.vector.memset(table_scales[:].bitcast(I32), 0)
+        for q in range(4):
+            nc.sync.dma_start(table_scales[32 * q : 32 * q + 4, :].bitcast(I32), tab_scales[0, 4 * q : 4 * q + 4, :].bitcast(I32))
+
+        w1_rows = w1.rearrange("(p j) r -> p j r", j=PACK)
+        w1_raw = [keep.tile([P, PACK, R // 2], F32, name=f"w1_raw{h}", tag=f"weights{h}") for h in range(2)]
+        for h in range(2):
+            nc.sync.dma_start(w1_raw[h][:], w1_rows[:, :, h * R // 2 : (h + 1) * R // 2])
+        table_words = keep.tile([P, T], U16, tag="words_then_res")
+        nc.sync.dma_start(table_words[:].bitcast(I32), tab_words[0].bitcast(I32))
+        offs2_sb = keep.tile([P, J // 16], U16)
+        nc.sync.dma_start(offs2_sb[:], offs2)
+        gain_sb = keep.tile([P, PACK], F32)
+        nc.gpsimd.dma_start(gain_sb[:], gain.rearrange("(p t) o -> p (t o)", t=PACK))
+        rs_sb = keep.tile([P, PACK], F32)
+        nc.gpsimd.dma_start(rs_sb[:], rs.rearrange("(p t) o -> p (t o)", t=PACK))
+
+        page = [keep.tile([P, U], F32, name=f"page{t}") for t in range(PACK)]
+        for t in range(PACK):
+            nc.vector.memset(page[t][:], 0.0)
+
+        w1_dealt = keep.tile([P, PACK, P, PACK], BF16, align_bytes=64)
+        deal(nc.vector.tensor_copy, w1_dealt, w1_raw[0], 0, 0, HALF)
+        picked_scales = keep.tile([P, J], U8, align_bytes=64)
+        nc.vector.tensor_copy(picked_scales[:], table_scales[:].indirect(offs_sb[:]))
+        deal(nc.vector.tensor_copy, w1_dealt, w1_raw[1], HALF, 0, W1_VECTOR_SHARE)
+        deal(nc.scalar.copy, w1_dealt, w1_raw[1], HALF, W1_VECTOR_SHARE, HALF)
+
+        ground_sb = keep.tile([P, PACK, U], F32, tag="scales_then_ground")
+        wor_rows = wor.rearrange("(p j) f -> p j f", j=PACK)
+        wor_raw = [keep.tile([P, PACK, F // 2], F32, name=f"wor_raw{h}", tag=f"weights{h}") for h in range(2)]
+        nc.sync.dma_start(wor_raw[0][:], wor_rows[:, :, : F // 2])
+        nc.sync.dma_start(ground_sb[:], ground.rearrange("(p t) u -> p t u", t=PACK))
+        nc.sync.dma_start(wor_raw[1][:], wor_rows[:, :, F // 2 :])
+
+        w1_codes = keep.tile([P, PACK, P], U32, align_bytes=64)
+        w1_scales = keep.tile([P, PACK, P], U8, align_bytes=64)
+        picked_words = keep.tile([P, J], U16, align_bytes=64)
+
+        def quantize_w1(t):
+            nc.vector.quantize_mx(
+                out=w1_codes[:, t, :].bitcast(FP8X4),
+                scales=w1_scales[:, t, :],
+                in_=w1_dealt[:, t, :, :].rearrange("p m j -> p (m j)"),
+            )
+
+        quantize_w1(0)
+        nc.vector.tensor_copy(picked_words[:], table_words[:].indirect(offs_sb[:]))
+        for t in range(1, PACK):
+            quantize_w1(t)
+        res_sb = keep.tile([P, PACK, U], F32, tag="words_then_res")
+        nc.sync.dma_start(res_sb[:], res.rearrange("(p t) u -> p t u", t=PACK))
+
+        h1 = [keep.tile([P, J], F32, name=f"h1_{t}") for t in range(PACK)]
+        for t in range(PACK):
+            a = psum.tile([P, J], F32, name=f"a{t}")
+            nc.tensor.matmul_mx(
+                out=a[:],
+                lhsT=w1_codes[:, t, :].bitcast(FP8X4),
+                lhsT_scale=w1_scales[:, t, :],
+                rhs=picked_words[:].bitcast(FP4X4),
+                rhs_scale=picked_scales[:],
+                start=True,
+                stop=True,
+            )
+            nc.scalar.activation(h1[t][:], a[:], COPY, scale=gain_sb[:, t : t + 1])
+
+        gate = [keep.tile([P, U], F32, name=f"gate{t}") for t in range(PACK)]
+        page_term = keep.tile([P, PACK, U], F32)
+        ground_term = keep.tile([P, PACK, U], F32)
+        wor_dealt = keep.tile([P, PACK, P, PACK], BF16, align_bytes=64)
+        wor_codes = keep.tile([P, PACK, P], U32, align_bytes=64)
+        wor_scales = keep.tile([P, PACK, P], U8, align_bytes=64)
+
+        def gate_ground(t):
+            nc.vector.scalar_tensor_tensor(ground_term[:, t, :], gate[t][:], rs_sb[:, t : t + 1], ground_sb[:, t, :], MULT, MULT)
+
+        for t in range(PACK):
+            nc.vector.tensor_copy(page[t][:].indirect(offs2_sb[:]), h1[t][:])
+            half, piece = divmod(t, 2)
+            deal(nc.scalar.copy, wor_dealt, wor_raw[half], half * HALF, piece * WOR_PIECE, (piece + 1) * WOR_PIECE)
+            nc.scalar.activation(gate[t][:], page[t][:], SIGMOID)
+            nc.scalar.activation(page_term[:, t, :], page[t][:], COPY, scale=rs_sb[:, t : t + 1])
+            if t > 0:
+                gate_ground(t - 1)
+        nc.vector.quantize_mx(
+            out=wor_codes[:].rearrange("p t m -> p (t m)").bitcast(FP8X4),
+            scales=wor_scales[:].rearrange("p t m -> p (t m)"),
+            in_=wor_dealt[:].rearrange("p t m j -> p (t m j)"),
+        )
+        gate_ground(PACK - 1)
+
+        fo1 = [keep.tile([P, PACK * CHUNK], BF16, name=f"fo1_{c}", align_bytes=64) for c in range(CHUNKS)]
+        fo1_codes = [keep.tile([P, CHUNK], U32, name=f"fo1_codes{c}", align_bytes=64) for c in range(CHUNKS)]
+        fo1_scales = [keep.tile([P, CHUNK], U8, name=f"fo1_scales{c}", align_bytes=64) for c in range(CHUNKS)]
+        yo = [psum.tile([P, PACK, CHUNK], F32, name=f"yo{c}") for c in range(CHUNKS)]
+        y = [keep.tile([P, PACK, CHUNK], F32, name=f"y{c}") for c in range(CHUNKS)]
+        y_words = [keep.tile([P, PACK * CHUNK], BF16, name=f"y_words{c}", align_bytes=64) for c in range(CHUNKS)]
+        y_codes = [keep.tile([P, CHUNK], U32, name=f"y_codes{c}", align_bytes=64) for c in range(CHUNKS)]
+        y_scales = keep.tile([P, U], U8, align_bytes=64)
+        out_rows = out_0.rearrange("(p t) u -> p t u", t=PACK)
+        out_words = out_1[0].rearrange("p c r -> p (c r)").bitcast(I32)
+
+        def cols(c):
+            return slice(c * CHUNK, (c + 1) * CHUNK)
+
+        def add_terms(c):
+            nc.vector.tensor_tensor(pairs_out(fo1[c][:]), pairs_in(page_term[:, :, cols(c)]), pairs_in(ground_term[:, :, cols(c)]), ADD)
+
+        def last_layer(c):
+            nc.vector.quantize_mx(out=fo1_codes[c][:].bitcast(FP8X4), scales=fo1_scales[c][:], in_=fo1[c][:])
+            for t in range(PACK):
+                nc.tensor.matmul_mx(
+                    out=yo[c][:, t, :],
+                    lhsT=wor_codes[:, t, :].bitcast(FP8X4),
+                    lhsT_scale=wor_scales[:, t, :],
+                    rhs=fo1_codes[c][:].bitcast(FP8X4),
+                    rhs_scale=fo1_scales[c][:],
+                    start=True,
+                    stop=True,
+                )
+
+        def add_residual(c):
+            nc.vector.tensor_tensor(y[c][:], yo[c][:], res_sb[:, :, cols(c)], ADD)
+            nc.sync.dma_start(out_rows[:, :, cols(c)], y[c][:])
+            nc.scalar.copy(pairs_out(y_words[c][:]), pairs_in(y[c][:]))
+
+        def hand_on(c):
+            nc.vector.quantize_mx(out=y_codes[c][:].bitcast(FP8X4), scales=y_scales[:, cols(c)], in_=y_words[c][:])
+            nc.sync.dma_start(out_words[:, cols(c)], y_codes[c][:].bitcast(I32))
+
+        stages = (add_terms, last_layer, None, add_residual, None, hand_on)
+        for step in range(CHUNKS + len(stages) - 1):
+            for lag, stage in enumerate(stages):
+                if stage is not None and 0 <= step - lag < CHUNKS:
+                    stage(step - lag)
+        for q in range(4):
+            queue = nc.scalar if q % 2 else nc.sync
+            queue.dma_start(out_2[0, 4 * q : 4 * q + 4, :].bitcast(I32), y_scales[32 * q : 32 * q + 4, :].bitcast(I32))

@@ -23,13 +23,12 @@ PACK = 4
 HALF = P // 2
 CHUNK = 128
 CHUNKS = U // CHUNK
-W1_VECTOR_SHARE = 44
 WOR_PIECE = 32
 
 
-def deal(copy, dealt, raw, first, m0, m1):
+def deal(copy, dealt, raw, m0, m1):
     copy(
-        dealt[:, :, first + m0 : first + m1, :].rearrange("p t m j -> p m j t"),
+        dealt[:, :, m0:m1, :].rearrange("p t m j -> p m j t"),
         raw[:, :, PACK * m0 : PACK * m1].rearrange("p j (m t) -> p m j t", t=PACK),
     )
 
@@ -50,20 +49,27 @@ def tile_attend_chgroundgate_pl_kernel(tc, tab_words, tab_scales, w1, gain, grou
 
         offs_sb = keep.tile([P, J // 16], U16)
         nc.sync.dma_start(offs_sb[:], offs)
-
-        table_scales = keep.tile([P, T], U8, tag="scales_then_ground")
-        nc.vector.memset(table_scales[:].bitcast(I32), 0)
-        for q in range(4):
-            nc.sync.dma_start(table_scales[32 * q : 32 * q + 4, :].bitcast(I32), tab_scales[0, 4 * q : 4 * q + 4, :].bitcast(I32))
-
         w1_rows = w1.rearrange("(p j) r -> p j r", j=PACK)
-        w1_raw = [keep.tile([P, PACK, R // 2], F32, name=f"w1_raw{h}", tag=f"weights{h}") for h in range(2)]
+        w1_raw = [keep.tile([P, PACK, R // 2], F32, name=f"w1_raw{h}", tag=f"w1_raw{h}") for h in range(2)]
         for h in range(2):
             nc.sync.dma_start(w1_raw[h][:], w1_rows[:, :, h * R // 2 : (h + 1) * R // 2])
-        table_words = keep.tile([P, T], U16, tag="words_then_res")
-        nc.sync.dma_start(table_words[:].bitcast(I32), tab_words[0].bitcast(I32))
         offs2_sb = keep.tile([P, J // 16], U16)
         nc.sync.dma_start(offs2_sb[:], offs2)
+        table_scales = keep.tile([P, T], U8)
+        nc.vector.memset(table_scales[:].bitcast(I32), 0)
+        scale_rows = tab_scales[0].bitcast(I32).rearrange("(q i) c -> i q c", i=4)
+        for i in range(4):
+            nc.sync.dma_start(table_scales[i:P:32, :].bitcast(I32), scale_rows[i])
+
+        warm_in = keep.tile([P, 1], F32, align_bytes=64, tag="table_words")
+        nc.vector.memset(warm_in[:], 0.0)
+        warm_out = keep.tile([P, 1], F32, tag="wor_raw")
+        nc.scalar.activation(warm_out[:], warm_in[:], SIGMOID)
+        table_words = keep.tile([P, T], U16, align_bytes=64, tag="table_words")
+        nc.sync.dma_start(table_words[:].bitcast(I32), tab_words[0].bitcast(I32))
+        wor_raw = keep.tile([P, PACK, F], F32, tag="wor_raw")
+        nc.sync.dma_start(wor_raw[:], wor.rearrange("(p j) f -> p j f", j=PACK))
+
         gain_sb = keep.tile([P, PACK], F32)
         nc.gpsimd.dma_start(gain_sb[:], gain.rearrange("(p t) o -> p (t o)", t=PACK))
         rs_sb = keep.tile([P, PACK], F32)
@@ -73,36 +79,38 @@ def tile_attend_chgroundgate_pl_kernel(tc, tab_words, tab_scales, w1, gain, grou
         for t in range(PACK):
             nc.vector.memset(page[t][:], 0.0)
 
-        w1_dealt = keep.tile([P, PACK, P, PACK], BF16, align_bytes=64)
-        deal(nc.vector.tensor_copy, w1_dealt, w1_raw[0], 0, 0, HALF)
-        picked_scales = keep.tile([P, J], U8, align_bytes=64)
-        nc.vector.tensor_copy(picked_scales[:], table_scales[:].indirect(offs_sb[:]))
-        deal(nc.vector.tensor_copy, w1_dealt, w1_raw[1], HALF, 0, W1_VECTOR_SHARE)
-        deal(nc.scalar.copy, w1_dealt, w1_raw[1], HALF, W1_VECTOR_SHARE, HALF)
+        w1_dealt = [keep.tile([P, 2, P, PACK], BF16, name=f"w1_dealt{pair}", tag=f"w1_dealt{pair}", align_bytes=64) for pair in range(2)]
+        for h in range(2):
+            for pair, copy in enumerate((nc.vector.tensor_copy, nc.scalar.copy)):
+                copy(
+                    w1_dealt[pair][:, :, h * HALF : (h + 1) * HALF, :].rearrange("p t m j -> p m j t"),
+                    w1_raw[h][:].rearrange("p j (m t) -> p m j t", t=PACK)[:, :, :, 2 * pair : 2 * pair + 2],
+                )
+        ground_rows = ground.rearrange("(p t) u -> p t u", t=PACK)
+        ground_sb = [keep.tile([P, 2, U], F32, name=f"ground{h}", tag=f"w1_raw{h}") for h in range(2)]
+        for h in range(2):
+            nc.sync.dma_start(ground_sb[h][:], ground_rows[:, 2 * h : 2 * h + 2, :])
 
-        ground_sb = keep.tile([P, PACK, U], F32, tag="scales_then_ground")
-        wor_rows = wor.rearrange("(p j) f -> p j f", j=PACK)
-        wor_raw = [keep.tile([P, PACK, F // 2], F32, name=f"wor_raw{h}", tag=f"weights{h}") for h in range(2)]
-        nc.sync.dma_start(wor_raw[0][:], wor_rows[:, :, : F // 2])
-        nc.sync.dma_start(ground_sb[:], ground.rearrange("(p t) u -> p t u", t=PACK))
-        nc.sync.dma_start(wor_raw[1][:], wor_rows[:, :, F // 2 :])
-
-        w1_codes = keep.tile([P, PACK, P], U32, align_bytes=64)
+        w1_first_codes = keep.tile([P, P], U32, align_bytes=64)
         w1_scales = keep.tile([P, PACK, P], U8, align_bytes=64)
+        picked_scales = keep.tile([P, J], U8, align_bytes=64)
         picked_words = keep.tile([P, J], U16, align_bytes=64)
 
-        def quantize_w1(t):
+        def quantize_w1(t, codes):
             nc.vector.quantize_mx(
-                out=w1_codes[:, t, :].bitcast(FP8X4),
+                out=codes.bitcast(FP8X4),
                 scales=w1_scales[:, t, :],
-                in_=w1_dealt[:, t, :, :].rearrange("p m j -> p (m j)"),
+                in_=w1_dealt[t // 2][:, t % 2, :, :].rearrange("p m j -> p (m j)"),
             )
 
-        quantize_w1(0)
+        quantize_w1(0, w1_first_codes[:])
+        nc.vector.tensor_copy(picked_scales[:], table_scales[:].indirect(offs_sb[:]))
         nc.vector.tensor_copy(picked_words[:], table_words[:].indirect(offs_sb[:]))
+        w1_later_codes = keep.tile([P, PACK - 1, P], U32, align_bytes=64, tag="table_words")
+        w1_codes = [w1_first_codes[:]] + [w1_later_codes[:, t, :] for t in range(PACK - 1)]
         for t in range(1, PACK):
-            quantize_w1(t)
-        res_sb = keep.tile([P, PACK, U], F32, tag="words_then_res")
+            quantize_w1(t, w1_codes[t])
+        res_sb = keep.tile([P, PACK, U], F32, align_bytes=64, tag="w1_dealt0")
         nc.sync.dma_start(res_sb[:], res.rearrange("(p t) u -> p t u", t=PACK))
 
         h1 = [keep.tile([P, J], F32, name=f"h1_{t}") for t in range(PACK)]
@@ -110,7 +118,7 @@ def tile_attend_chgroundgate_pl_kernel(tc, tab_words, tab_scales, w1, gain, grou
             a = psum.tile([P, J], F32, name=f"a{t}")
             nc.tensor.matmul_mx(
                 out=a[:],
-                lhsT=w1_codes[:, t, :].bitcast(FP8X4),
+                lhsT=w1_codes[t].bitcast(FP8X4),
                 lhsT_scale=w1_scales[:, t, :],
                 rhs=picked_words[:].bitcast(FP4X4),
                 rhs_scale=picked_scales[:],
@@ -122,17 +130,16 @@ def tile_attend_chgroundgate_pl_kernel(tc, tab_words, tab_scales, w1, gain, grou
         gate = [keep.tile([P, U], F32, name=f"gate{t}") for t in range(PACK)]
         page_term = keep.tile([P, PACK, U], F32)
         ground_term = keep.tile([P, PACK, U], F32)
-        wor_dealt = keep.tile([P, PACK, P, PACK], BF16, align_bytes=64)
+        wor_dealt = keep.tile([P, PACK, P, PACK], BF16, align_bytes=64, tag="table_words")
         wor_codes = keep.tile([P, PACK, P], U32, align_bytes=64)
         wor_scales = keep.tile([P, PACK, P], U8, align_bytes=64)
 
         def gate_ground(t):
-            nc.vector.scalar_tensor_tensor(ground_term[:, t, :], gate[t][:], rs_sb[:, t : t + 1], ground_sb[:, t, :], MULT, MULT)
+            nc.vector.scalar_tensor_tensor(ground_term[:, t, :], gate[t][:], rs_sb[:, t : t + 1], ground_sb[t // 2][:, t % 2, :], MULT, MULT)
 
         for t in range(PACK):
             nc.vector.tensor_copy(page[t][:].indirect(offs2_sb[:]), h1[t][:])
-            half, piece = divmod(t, 2)
-            deal(nc.scalar.copy, wor_dealt, wor_raw[half], half * HALF, piece * WOR_PIECE, (piece + 1) * WOR_PIECE)
+            deal(nc.scalar.copy, wor_dealt[:], wor_raw[:], t * WOR_PIECE, (t + 1) * WOR_PIECE)
             nc.scalar.activation(gate[t][:], page[t][:], SIGMOID)
             nc.scalar.activation(page_term[:, t, :], page[t][:], COPY, scale=rs_sb[:, t : t + 1])
             if t > 0:
@@ -150,7 +157,7 @@ def tile_attend_chgroundgate_pl_kernel(tc, tab_words, tab_scales, w1, gain, grou
         yo = [psum.tile([P, PACK, CHUNK], F32, name=f"yo{c}") for c in range(CHUNKS)]
         y = [keep.tile([P, PACK, CHUNK], F32, name=f"y{c}") for c in range(CHUNKS)]
         y_words = [keep.tile([P, PACK * CHUNK], BF16, name=f"y_words{c}", align_bytes=64) for c in range(CHUNKS)]
-        y_codes = [keep.tile([P, CHUNK], U32, name=f"y_codes{c}", align_bytes=64) for c in range(CHUNKS)]
+        y_codes = [keep.tile([P, 2 * CHUNK], U32, name=f"y_codes{h}", align_bytes=64) for h in range(CHUNKS // 2)]
         y_scales = keep.tile([P, U], U8, align_bytes=64)
         out_rows = out_0.rearrange("(p t) u -> p t u", t=PACK)
         out_words = out_1[0].rearrange("p c r -> p (c r)").bitcast(I32)
@@ -180,14 +187,17 @@ def tile_attend_chgroundgate_pl_kernel(tc, tab_words, tab_scales, w1, gain, grou
             nc.scalar.copy(pairs_out(y_words[c][:]), pairs_in(y[c][:]))
 
         def hand_on(c):
-            nc.vector.quantize_mx(out=y_codes[c][:].bitcast(FP8X4), scales=y_scales[:, cols(c)], in_=y_words[c][:])
-            nc.sync.dma_start(out_words[:, cols(c)], y_codes[c][:].bitcast(I32))
+            h, second = divmod(c, 2)
+            nc.vector.quantize_mx(out=y_codes[h][:, cols(second)].bitcast(FP8X4), scales=y_scales[:, cols(c)], in_=y_words[c][:])
+            if second:
+                nc.sync.dma_start(out_words[:, 2 * h * CHUNK : 2 * (h + 1) * CHUNK], y_codes[h][:].bitcast(I32))
 
         stages = (add_terms, last_layer, None, add_residual, None, hand_on)
         for step in range(CHUNKS + len(stages) - 1):
             for lag, stage in enumerate(stages):
                 if stage is not None and 0 <= step - lag < CHUNKS:
                     stage(step - lag)
-        for q in range(4):
-            queue = nc.scalar if q % 2 else nc.sync
-            queue.dma_start(out_2[0, 4 * q : 4 * q + 4, :].bitcast(I32), y_scales[32 * q : 32 * q + 4, :].bitcast(I32))
+        out_scale_rows = out_2[0].bitcast(I32).rearrange("(q i) c -> i q c", i=4)
+        for i in range(4):
+            queue = nc.scalar if i % 2 else nc.sync
+            queue.dma_start(out_scale_rows[i], y_scales[i:P:32, :].bitcast(I32))

@@ -24,6 +24,7 @@ HALF = P // 2
 CHUNK = 128
 CHUNKS = U // CHUNK
 WOR_PIECE = 32
+GPSIMD_PLACES = 2
 
 
 def deal(copy, dealt, raw, m0, m1):
@@ -134,14 +135,24 @@ def tile_attend_chgroundgate_pl_kernel(tc, tab_words, tab_scales, w1, gain, grou
         wor_codes = keep.tile([P, PACK, P], U32, align_bytes=64)
         wor_scales = keep.tile([P, PACK, P], U8, align_bytes=64)
 
+        scaled_ground = [keep.tile([P, U], F32, name=f"scaled_ground{t}") for t in range(GPSIMD_PLACES)]
+        for t in range(GPSIMD_PLACES):
+            nc.gpsimd.tensor_scalar(scaled_ground[t][:], ground_sb[t // 2][:, t % 2, :], rs_sb[:, t : t + 1], 0.0, MULT, ADD)
+
         def gate_ground(t):
-            nc.vector.scalar_tensor_tensor(ground_term[:, t, :], gate[t][:], rs_sb[:, t : t + 1], ground_sb[t // 2][:, t % 2, :], MULT, MULT)
+            if t < GPSIMD_PLACES:
+                nc.gpsimd.tensor_tensor(ground_term[:, t, :], gate[t][:], scaled_ground[t][:], MULT)
+            else:
+                nc.vector.scalar_tensor_tensor(ground_term[:, t, :], gate[t][:], rs_sb[:, t : t + 1], ground_sb[t // 2][:, t % 2, :], MULT, MULT)
 
         for t in range(PACK):
             nc.vector.tensor_copy(page[t][:].indirect(offs2_sb[:]), h1[t][:])
             deal(nc.scalar.copy, wor_dealt[:], wor_raw[:], t * WOR_PIECE, (t + 1) * WOR_PIECE)
             nc.scalar.activation(gate[t][:], page[t][:], SIGMOID)
-            nc.scalar.activation(page_term[:, t, :], page[t][:], COPY, scale=rs_sb[:, t : t + 1])
+            if t == 0:
+                nc.gpsimd.tensor_scalar(page_term[:, t, :], page[t][:], rs_sb[:, t : t + 1], 0.0, MULT, ADD)
+            else:
+                nc.scalar.activation(page_term[:, t, :], page[t][:], COPY, scale=rs_sb[:, t : t + 1])
             if t > 0:
                 gate_ground(t - 1)
         nc.vector.quantize_mx(

@@ -56,7 +56,7 @@ def tile_attend_chgroundgate_pl_kernel(tc, tab_words, tab_scales, w1, gain, grou
             nc.sync.dma_start(w1_raw[h][:], w1_rows[:, :, h * R // 2 : (h + 1) * R // 2])
         offs2_sb = keep.tile([P, J // 16], U16)
         nc.sync.dma_start(offs2_sb[:], offs2)
-        table_scales = keep.tile([P, T], U8)
+        table_scales = keep.tile([P, T], U8, tag="table_scales")
         nc.vector.memset(table_scales[:].bitcast(I32), 0)
         scale_rows = tab_scales[0].bitcast(I32).rearrange("(q i) c -> i q c", i=4)
         for i in range(4):
@@ -64,12 +64,13 @@ def tile_attend_chgroundgate_pl_kernel(tc, tab_words, tab_scales, w1, gain, grou
 
         warm_in = keep.tile([P, 1], F32, align_bytes=64, tag="table_words")
         nc.vector.memset(warm_in[:], 0.0)
-        warm_out = keep.tile([P, 1], F32, tag="wor_raw")
+        warm_out = keep.tile([P, 1], F32, tag="ground0")
         nc.scalar.activation(warm_out[:], warm_in[:], SIGMOID)
         table_words = keep.tile([P, T], U16, align_bytes=64, tag="table_words")
         nc.sync.dma_start(table_words[:].bitcast(I32), tab_words[0].bitcast(I32))
-        wor_raw = keep.tile([P, PACK, F], F32, tag="wor_raw")
-        nc.sync.dma_start(wor_raw[:], wor.rearrange("(p j) f -> p j f", j=PACK))
+        ground_rows = ground.rearrange("(p t) u -> p t u", t=PACK)
+        ground_first = keep.tile([P, 2, U], F32, tag="ground0")
+        nc.sync.dma_start(ground_first[:], ground_rows[:, :2, :])
 
         gain_sb = keep.tile([P, PACK], F32)
         nc.gpsimd.dma_start(gain_sb[:], gain.rearrange("(p t) o -> p (t o)", t=PACK))
@@ -87,10 +88,10 @@ def tile_attend_chgroundgate_pl_kernel(tc, tab_words, tab_scales, w1, gain, grou
                     w1_dealt[pair][:, :, h * HALF : (h + 1) * HALF, :].rearrange("p t m j -> p m j t"),
                     w1_raw[h][:].rearrange("p j (m t) -> p m j t", t=PACK)[:, :, :, 2 * pair : 2 * pair + 2],
                 )
-        ground_rows = ground.rearrange("(p t) u -> p t u", t=PACK)
-        ground_sb = [keep.tile([P, 2, U], F32, name=f"ground{h}", tag=f"w1_raw{h}") for h in range(2)]
+        wor_rows = wor.rearrange("(p j) f -> p j f", j=PACK)
+        wor_raw = [keep.tile([P, PACK, F // 2], F32, name=f"wor_raw{h}", tag=f"w1_raw{h}") for h in range(2)]
         for h in range(2):
-            nc.sync.dma_start(ground_sb[h][:], ground_rows[:, 2 * h : 2 * h + 2, :])
+            nc.sync.dma_start(wor_raw[h][:], wor_rows[:, :, h * F // 2 : (h + 1) * F // 2])
 
         w1_first_codes = keep.tile([P, P], U32, align_bytes=64)
         w1_scales = keep.tile([P, PACK, P], U8, align_bytes=64)
@@ -106,6 +107,9 @@ def tile_attend_chgroundgate_pl_kernel(tc, tab_words, tab_scales, w1, gain, grou
 
         quantize_w1(0, w1_first_codes[:])
         nc.vector.tensor_copy(picked_scales[:], table_scales[:].indirect(offs_sb[:]))
+        ground_second = keep.tile([P, 2, U], F32, tag="table_scales")
+        nc.sync.dma_start(ground_second[:], ground_rows[:, 2:, :])
+        ground_sb = (ground_first, ground_second)
         nc.vector.tensor_copy(picked_words[:], table_words[:].indirect(offs_sb[:]))
         w1_later_codes = keep.tile([P, PACK - 1, P], U32, align_bytes=64, tag="table_words")
         w1_codes = [w1_first_codes[:]] + [w1_later_codes[:, t, :] for t in range(PACK - 1)]
@@ -128,8 +132,6 @@ def tile_attend_chgroundgate_pl_kernel(tc, tab_words, tab_scales, w1, gain, grou
             )
             nc.scalar.activation(h1[t][:], a[:], COPY, scale=gain_sb[:, t : t + 1])
 
-        gate = [keep.tile([P, U], F32, name=f"gate{t}") for t in range(PACK)]
-        page_term = keep.tile([P, PACK, U], F32)
         ground_term = keep.tile([P, PACK, U], F32)
         wor_dealt = keep.tile([P, PACK, P, PACK], BF16, align_bytes=64, tag="table_words")
         wor_codes = keep.tile([P, PACK, P], U32, align_bytes=64)
@@ -139,22 +141,37 @@ def tile_attend_chgroundgate_pl_kernel(tc, tab_words, tab_scales, w1, gain, grou
         for t in range(GPSIMD_PLACES):
             nc.gpsimd.tensor_scalar(scaled_ground[t][:], ground_sb[t // 2][:, t % 2, :], rs_sb[:, t : t + 1], 0.0, MULT, ADD)
 
-        def gate_ground(t):
-            if t < GPSIMD_PLACES:
-                nc.gpsimd.tensor_tensor(ground_term[:, t, :], gate[t][:], scaled_ground[t][:], MULT)
-            else:
-                nc.vector.scalar_tensor_tensor(ground_term[:, t, :], gate[t][:], rs_sb[:, t : t + 1], ground_sb[t // 2][:, t % 2, :], MULT, MULT)
-
-        for t in range(PACK):
+        def scatter(t):
             nc.vector.tensor_copy(page[t][:].indirect(offs2_sb[:]), h1[t][:])
-            deal(nc.scalar.copy, wor_dealt[:], wor_raw[:], t * WOR_PIECE, (t + 1) * WOR_PIECE)
-            nc.scalar.activation(gate[t][:], page[t][:], SIGMOID)
-            if t == 0:
-                nc.gpsimd.tensor_scalar(page_term[:, t, :], page[t][:], rs_sb[:, t : t + 1], 0.0, MULT, ADD)
-            else:
-                nc.scalar.activation(page_term[:, t, :], page[t][:], COPY, scale=rs_sb[:, t : t + 1])
-            if t > 0:
-                gate_ground(t - 1)
+
+        def deal_wor(piece):
+            half, first = divmod(piece * WOR_PIECE, HALF)
+            deal(nc.scalar.copy, wor_dealt[:, :, half * HALF : (half + 1) * HALF, :], wor_raw[half][:], first, first + WOR_PIECE)
+
+        gate = []
+        for t in range(GPSIMD_PLACES):
+            scatter(t)
+            deal_wor(t)
+            gate_tile = keep.tile([P, U], F32, name=f"gate{t}", tag=("gate0", "w1_raw0")[t])
+            gate.append(gate_tile[:])
+            nc.scalar.activation(gate[t], page[t][:], SIGMOID)
+            nc.gpsimd.tensor_tensor(ground_term[:, t, :], gate[t], scaled_ground[t][:], MULT)
+        for piece in range(GPSIMD_PLACES, PACK):
+            deal_wor(piece)
+        late = keep.tile([P, PACK + 2, U], F32, tag="w1_raw1")
+        page_term = late[:, :PACK, :]
+        gate.extend(late[:, PACK + i, :] for i in range(2))
+        nc.gpsimd.tensor_scalar(page_term[:, 0, :], page[0][:], rs_sb[:, 0:1], 0.0, MULT, ADD)
+        nc.scalar.activation(page_term[:, 1, :], page[1][:], COPY, scale=rs_sb[:, 1:2])
+
+        def gate_ground(t):
+            nc.vector.scalar_tensor_tensor(ground_term[:, t, :], gate[t], rs_sb[:, t : t + 1], ground_sb[t // 2][:, t % 2, :], MULT, MULT)
+
+        for t in range(GPSIMD_PLACES, PACK):
+            scatter(t)
+            nc.scalar.activation(gate[t], page[t][:], SIGMOID)
+            nc.scalar.activation(page_term[:, t, :], page[t][:], COPY, scale=rs_sb[:, t : t + 1])
+        gate_ground(PACK - 2)
         nc.vector.quantize_mx(
             out=wor_codes[:].rearrange("p t m -> p (t m)").bitcast(FP8X4),
             scales=wor_scales[:].rearrange("p t m -> p (t m)"),

@@ -20,18 +20,22 @@ SIGMOID = mybir.ActivationFunctionType.Sigmoid
 
 P = 128
 PACK = 4
+QUADRANT = 32
+SCALE_ROWS = 4
+LIST_GROUP = 16
 HALF = P // 2
 CHUNK = 128
 CHUNKS = U // CHUNK
-WOR_PIECE = 32
-GPSIMD_PLACES = 2
+WOR_PIECE = P // PACK
+EARLY_PLACES = 2
 
 
-def deal(copy, dealt, raw, m0, m1):
-    copy(
-        dealt[:, :, m0:m1, :].rearrange("p t m j -> p m j t"),
-        raw[:, :, PACK * m0 : PACK * m1].rearrange("p j (m t) -> p m j t", t=PACK),
-    )
+def deal(copy, dealt, raw):
+    copy(dealt.rearrange("p t m j -> p m j t"), raw)
+
+
+def by_place(raw):
+    return raw.rearrange("p j (m t) -> p m j t", t=PACK)
 
 
 def pairs_out(words):
@@ -48,29 +52,30 @@ def tile_attend_chgroundgate_pl_kernel(tc, tab_words, tab_scales, w1, gain, grou
         keep = ctx.enter_context(tc.tile_pool(name="keep", bufs=1))
         psum = ctx.enter_context(tc.psum_pool(name="psum", bufs=1))
 
-        offs_sb = keep.tile([P, J // 16], U16)
+        offs_sb = keep.tile([P, J // LIST_GROUP], U16)
         nc.sync.dma_start(offs_sb[:], offs)
         w1_rows = w1.rearrange("(p j) r -> p j r", j=PACK)
         w1_raw = [keep.tile([P, PACK, R // 2], F32, name=f"w1_raw{h}", tag=f"w1_raw{h}") for h in range(2)]
         for h in range(2):
             nc.sync.dma_start(w1_raw[h][:], w1_rows[:, :, h * R // 2 : (h + 1) * R // 2])
-        offs2_sb = keep.tile([P, J // 16], U16)
+        offs2_sb = keep.tile([P, J // LIST_GROUP], U16)
         nc.sync.dma_start(offs2_sb[:], offs2)
+
         table_scales = keep.tile([P, T], U8, tag="table_scales")
         nc.vector.memset(table_scales[:].bitcast(I32), 0)
-        scale_rows = tab_scales[0].bitcast(I32).rearrange("(q i) c -> i q c", i=4)
-        for i in range(4):
-            nc.sync.dma_start(table_scales[i:P:32, :].bitcast(I32), scale_rows[i])
+        scale_rows = tab_scales[0].bitcast(I32).rearrange("(q i) c -> i q c", i=SCALE_ROWS)
+        for i in range(SCALE_ROWS):
+            nc.sync.dma_start(table_scales[i:P:QUADRANT, :].bitcast(I32), scale_rows[i])
 
         warm_in = keep.tile([P, 1], F32, align_bytes=64, tag="table_words")
         nc.vector.memset(warm_in[:], 0.0)
-        warm_out = keep.tile([P, 1], F32, tag="ground0")
+        warm_out = keep.tile([P, 1], F32, tag="wor_first")
         nc.scalar.activation(warm_out[:], warm_in[:], SIGMOID)
         table_words = keep.tile([P, T], U16, align_bytes=64, tag="table_words")
         nc.sync.dma_start(table_words[:].bitcast(I32), tab_words[0].bitcast(I32))
-        ground_rows = ground.rearrange("(p t) u -> p t u", t=PACK)
-        ground_first = keep.tile([P, 2, U], F32, tag="ground0")
-        nc.sync.dma_start(ground_first[:], ground_rows[:, :2, :])
+        wor_rows = wor.rearrange("(p j) f -> p j f", j=PACK)
+        wor_first = keep.tile([P, PACK, F // 2], F32, tag="wor_first")
+        nc.sync.dma_start(wor_first[:], wor_rows[:, :, : F // 2])
 
         gain_sb = keep.tile([P, PACK], F32)
         nc.gpsimd.dma_start(gain_sb[:], gain.rearrange("(p t) o -> p (t o)", t=PACK))
@@ -84,14 +89,14 @@ def tile_attend_chgroundgate_pl_kernel(tc, tab_words, tab_scales, w1, gain, grou
         w1_dealt = [keep.tile([P, 2, P, PACK], BF16, name=f"w1_dealt{pair}", tag=f"w1_dealt{pair}", align_bytes=64) for pair in range(2)]
         for h in range(2):
             for pair, copy in enumerate((nc.vector.tensor_copy, nc.scalar.copy)):
-                copy(
-                    w1_dealt[pair][:, :, h * HALF : (h + 1) * HALF, :].rearrange("p t m j -> p m j t"),
-                    w1_raw[h][:].rearrange("p j (m t) -> p m j t", t=PACK)[:, :, :, 2 * pair : 2 * pair + 2],
-                )
-        wor_rows = wor.rearrange("(p j) f -> p j f", j=PACK)
-        wor_raw = [keep.tile([P, PACK, F // 2], F32, name=f"wor_raw{h}", tag=f"w1_raw{h}") for h in range(2)]
-        for h in range(2):
-            nc.sync.dma_start(wor_raw[h][:], wor_rows[:, :, h * F // 2 : (h + 1) * F // 2])
+                deal(copy, w1_dealt[pair][:, :, h * HALF : (h + 1) * HALF, :], by_place(w1_raw[h][:])[:, :, :, 2 * pair : 2 * pair + 2])
+
+        ground_rows = ground.rearrange("(p t) u -> p t u", t=PACK)
+        ground_early = keep.tile([P, EARLY_PLACES, U], F32, tag="w1_raw0")
+        nc.sync.dma_start(ground_early[:], ground_rows[:, :EARLY_PLACES, :])
+        wor_second = keep.tile([P, PACK, F // 2], F32, tag="w1_raw1")
+        nc.sync.dma_start(wor_second[:], wor_rows[:, :, F // 2 :])
+        wor_raw = (wor_first, wor_second)
 
         w1_first_codes = keep.tile([P, P], U32, align_bytes=64)
         w1_scales = keep.tile([P, PACK, P], U8, align_bytes=64)
@@ -107,9 +112,8 @@ def tile_attend_chgroundgate_pl_kernel(tc, tab_words, tab_scales, w1, gain, grou
 
         quantize_w1(0, w1_first_codes[:])
         nc.vector.tensor_copy(picked_scales[:], table_scales[:].indirect(offs_sb[:]))
-        ground_second = keep.tile([P, 2, U], F32, tag="table_scales")
-        nc.sync.dma_start(ground_second[:], ground_rows[:, 2:, :])
-        ground_sb = (ground_first, ground_second)
+        ground_late = keep.tile([P, PACK - EARLY_PLACES, U], F32, tag="table_scales")
+        nc.sync.dma_start(ground_late[:], ground_rows[:, EARLY_PLACES:, :])
         nc.vector.tensor_copy(picked_words[:], table_words[:].indirect(offs_sb[:]))
         w1_later_codes = keep.tile([P, PACK - 1, P], U32, align_bytes=64, tag="table_words")
         w1_codes = [w1_first_codes[:]] + [w1_later_codes[:, t, :] for t in range(PACK - 1)]
@@ -137,55 +141,60 @@ def tile_attend_chgroundgate_pl_kernel(tc, tab_words, tab_scales, w1, gain, grou
         wor_codes = keep.tile([P, PACK, P], U32, align_bytes=64)
         wor_scales = keep.tile([P, PACK, P], U8, align_bytes=64)
 
-        scaled_ground = [keep.tile([P, U], F32, name=f"scaled_ground{t}") for t in range(GPSIMD_PLACES)]
-        for t in range(GPSIMD_PLACES):
-            nc.gpsimd.tensor_scalar(scaled_ground[t][:], ground_sb[t // 2][:, t % 2, :], rs_sb[:, t : t + 1], 0.0, MULT, ADD)
+        ground_rs = [keep.tile([P, U], F32, name=f"ground_rs{t}") for t in range(EARLY_PLACES)]
+        for t in range(EARLY_PLACES):
+            nc.gpsimd.tensor_scalar(ground_rs[t][:], ground_early[:, t, :], rs_sb[:, t : t + 1], 0.0, MULT, ADD)
 
         def scatter(t):
             nc.vector.tensor_copy(page[t][:].indirect(offs2_sb[:]), h1[t][:])
 
         def deal_wor(piece):
-            half, first = divmod(piece * WOR_PIECE, HALF)
-            deal(nc.scalar.copy, wor_dealt[:, :, half * HALF : (half + 1) * HALF, :], wor_raw[half][:], first, first + WOR_PIECE)
+            h, first = divmod(piece * WOR_PIECE, HALF)
+            m0 = piece * WOR_PIECE
+            deal(nc.scalar.copy, wor_dealt[:, :, m0 : m0 + WOR_PIECE, :], by_place(wor_raw[h][:, :, PACK * first : PACK * (first + WOR_PIECE)]))
 
         gate = []
-        for t in range(GPSIMD_PLACES):
+        for t, tag in enumerate(("gate0", "wor_first")):
             scatter(t)
             deal_wor(t)
-            gate_tile = keep.tile([P, U], F32, name=f"gate{t}", tag=("gate0", "w1_raw0")[t])
-            gate.append(gate_tile[:])
+            early_gate = keep.tile([P, U], F32, name=f"gate{t}", tag=tag)
+            gate.append(early_gate[:])
             nc.scalar.activation(gate[t], page[t][:], SIGMOID)
-            nc.gpsimd.tensor_tensor(ground_term[:, t, :], gate[t], scaled_ground[t][:], MULT)
-        for piece in range(GPSIMD_PLACES, PACK):
+            nc.gpsimd.tensor_tensor(ground_term[:, t, :], gate[t], ground_rs[t][:], MULT)
+        for piece in range(EARLY_PLACES, PACK):
             deal_wor(piece)
-        late = keep.tile([P, PACK + 2, U], F32, tag="w1_raw1")
+
+        late = keep.tile([P, 2 * PACK - EARLY_PLACES, U], F32, tag="w1_raw1")
         page_term = late[:, :PACK, :]
-        gate.extend(late[:, PACK + i, :] for i in range(2))
-        nc.gpsimd.tensor_scalar(page_term[:, 0, :], page[0][:], rs_sb[:, 0:1], 0.0, MULT, ADD)
-        nc.scalar.activation(page_term[:, 1, :], page[1][:], COPY, scale=rs_sb[:, 1:2])
+        gate.extend(late[:, PACK + i, :] for i in range(PACK - EARLY_PLACES))
 
-        def gate_ground(t):
-            nc.vector.scalar_tensor_tensor(ground_term[:, t, :], gate[t], rs_sb[:, t : t + 1], ground_sb[t // 2][:, t % 2, :], MULT, MULT)
+        def page_term_on_scalar(t):
+            nc.scalar.activation(page_term[:, t, :], page[t][:], COPY, scale=rs_sb[:, t : t + 1])
 
-        for t in range(GPSIMD_PLACES, PACK):
+        def ground_term_on_vector(t):
+            nc.vector.scalar_tensor_tensor(ground_term[:, t, :], gate[t], rs_sb[:, t : t + 1], ground_late[:, t - EARLY_PLACES, :], MULT, MULT)
+
+        nc.vector.tensor_scalar(page_term[:, 0, :], page[0][:], rs_sb[:, 0:1], None, MULT)
+        page_term_on_scalar(1)
+        for t in range(EARLY_PLACES, PACK):
             scatter(t)
             nc.scalar.activation(gate[t], page[t][:], SIGMOID)
-            nc.scalar.activation(page_term[:, t, :], page[t][:], COPY, scale=rs_sb[:, t : t + 1])
-        gate_ground(PACK - 2)
+            page_term_on_scalar(t)
+        ground_term_on_vector(PACK - 2)
         nc.vector.quantize_mx(
             out=wor_codes[:].rearrange("p t m -> p (t m)").bitcast(FP8X4),
             scales=wor_scales[:].rearrange("p t m -> p (t m)"),
             in_=wor_dealt[:].rearrange("p t m j -> p (t m j)"),
         )
-        gate_ground(PACK - 1)
+        ground_term_on_vector(PACK - 1)
 
         fo1 = [keep.tile([P, PACK * CHUNK], BF16, name=f"fo1_{c}", align_bytes=64) for c in range(CHUNKS)]
         fo1_codes = [keep.tile([P, CHUNK], U32, name=f"fo1_codes{c}", align_bytes=64) for c in range(CHUNKS)]
         fo1_scales = [keep.tile([P, CHUNK], U8, name=f"fo1_scales{c}", align_bytes=64) for c in range(CHUNKS)]
         yo = [psum.tile([P, PACK, CHUNK], F32, name=f"yo{c}") for c in range(CHUNKS)]
         y = [keep.tile([P, PACK, CHUNK], F32, name=f"y{c}") for c in range(CHUNKS)]
-        y_words = [keep.tile([P, PACK * CHUNK], BF16, name=f"y_words{c}", align_bytes=64) for c in range(CHUNKS)]
-        y_codes = [keep.tile([P, 2 * CHUNK], U32, name=f"y_codes{h}", align_bytes=64) for h in range(CHUNKS // 2)]
+        y_rounded = [keep.tile([P, PACK * CHUNK], BF16, name=f"y_rounded{c}", align_bytes=64) for c in range(CHUNKS)]
+        y_codes = [keep.tile([P, 2 * CHUNK], U32, name=f"y_codes{g}", align_bytes=64) for g in range(CHUNKS // 2)]
         y_scales = keep.tile([P, U], U8, align_bytes=64)
         out_rows = out_0.rearrange("(p t) u -> p t u", t=PACK)
         out_words = out_1[0].rearrange("p c r -> p (c r)").bitcast(I32)
@@ -212,20 +221,21 @@ def tile_attend_chgroundgate_pl_kernel(tc, tab_words, tab_scales, w1, gain, grou
         def add_residual(c):
             nc.vector.tensor_tensor(y[c][:], yo[c][:], res_sb[:, :, cols(c)], ADD)
             nc.sync.dma_start(out_rows[:, :, cols(c)], y[c][:])
-            nc.scalar.copy(pairs_out(y_words[c][:]), pairs_in(y[c][:]))
+            nc.scalar.copy(pairs_out(y_rounded[c][:]), pairs_in(y[c][:]))
 
         def hand_on(c):
-            h, second = divmod(c, 2)
-            nc.vector.quantize_mx(out=y_codes[h][:, cols(second)].bitcast(FP8X4), scales=y_scales[:, cols(c)], in_=y_words[c][:])
+            g, second = divmod(c, 2)
+            nc.vector.quantize_mx(out=y_codes[g][:, cols(second)].bitcast(FP8X4), scales=y_scales[:, cols(c)], in_=y_rounded[c][:])
             if second:
-                nc.sync.dma_start(out_words[:, 2 * h * CHUNK : 2 * (h + 1) * CHUNK], y_codes[h][:].bitcast(I32))
+                nc.sync.dma_start(out_words[:, 2 * g * CHUNK : 2 * (g + 1) * CHUNK], y_codes[g][:].bitcast(I32))
 
-        stages = (add_terms, last_layer, None, add_residual, None, hand_on)
-        for step in range(CHUNKS + len(stages) - 1):
-            for lag, stage in enumerate(stages):
-                if stage is not None and 0 <= step - lag < CHUNKS:
+        stages = ((add_terms, 0), (last_layer, 1), (add_residual, 3), (hand_on, 5))
+        for step in range(CHUNKS + stages[-1][1]):
+            for stage, lag in stages:
+                if 0 <= step - lag < CHUNKS:
                     stage(step - lag)
-        out_scale_rows = out_2[0].bitcast(I32).rearrange("(q i) c -> i q c", i=4)
-        for i in range(4):
+
+        out_scale_rows = out_2[0].bitcast(I32).rearrange("(q i) c -> i q c", i=SCALE_ROWS)
+        for i in range(SCALE_ROWS):
             queue = nc.scalar if i % 2 else nc.sync
-            queue.dma_start(out_scale_rows[i], y_scales[i:P:32, :].bitcast(I32))
+            queue.dma_start(out_scale_rows[i], y_scales[i:P:QUADRANT, :].bitcast(I32))

from contextlib import ExitStack

import concourse.mybir as mybir

K, R, F, T, J, U = 512, 512, 512, 2048, 256, 512
FLOPS = 2 * K * R * J + 2 * R * F * U

F32 = mybir.dt.float32
BF16 = mybir.dt.bfloat16
I32 = mybir.dt.int32
U32 = mybir.dt.uint32
U16 = mybir.dt.uint16
U8 = mybir.dt.uint8
FP8X4 = mybir.dt.float8_e4m3fn_x4
FP4X4 = mybir.dt.float4_e2m1fn_x4
MULT = mybir.AluOpType.mult
ADD = mybir.AluOpType.add
COPY = mybir.ActivationFunctionType.Copy
SIGMOID = mybir.ActivationFunctionType.Sigmoid

P = 128
PACK = 4
QUADRANT = 32
SCALE_ROWS = 4
LIST_GROUP = 16
HALF = P // 2
CHUNK = 128
CHUNKS = U // CHUNK
WOR_PIECE = P // PACK
EARLY_PLACES = 2


def deal(copy, dealt, raw):
    copy(dealt.rearrange("p t m j -> p m j t"), raw)


def by_place(raw):
    return raw.rearrange("p j (m t) -> p m j t", t=PACK)


def pairs_out(words):
    return words.rearrange("p (c i t) -> p c t i", i=2, t=PACK)


def pairs_in(rows):
    return rows.rearrange("p t (c i) -> p c t i", i=2)


def tile_attend_chgroundgate_pl_kernel(tc, tab_words, tab_scales, w1, gain, ground, rs, wor, res, offs, offs2, out_0, out_1, out_2):
    nc = tc.nc
    with ExitStack() as ctx:
        keep = ctx.enter_context(tc.tile_pool(name="keep", bufs=1))
        psum = ctx.enter_context(tc.psum_pool(name="psum", bufs=1))

        offs_sb = keep.tile([P, J // LIST_GROUP], U16)
        nc.sync.dma_start(offs_sb[:], offs)
        w1_rows = w1.rearrange("(p j) r -> p j r", j=PACK)
        w1_raw = [keep.tile([P, PACK, R // 2], F32, name=f"w1_raw{h}", tag=f"w1_raw{h}") for h in range(2)]
        for h in range(2):
            nc.sync.dma_start(w1_raw[h][:], w1_rows[:, :, h * R // 2 : (h + 1) * R // 2])
        offs2_sb = keep.tile([P, J // LIST_GROUP], U16)
        nc.sync.dma_start(offs2_sb[:], offs2)

        table_scales = keep.tile([P, T], U8, tag="table_scales")
        nc.vector.memset(table_scales[:].bitcast(I32), 0)
        scale_rows = tab_scales[0].bitcast(I32).rearrange("(q i) c -> i q c", i=SCALE_ROWS)
        for i in range(SCALE_ROWS):
            nc.sync.dma_start(table_scales[i:P:QUADRANT, :].bitcast(I32), scale_rows[i])

        warm_in = keep.tile([P, 1], F32, align_bytes=64, tag="table_words")
        nc.vector.memset(warm_in[:], 0.0)
        warm_out = keep.tile([P, 1], F32, tag="wor_first")
        nc.scalar.activation(warm_out[:], warm_in[:], SIGMOID)
        table_words = keep.tile([P, T], U16, align_bytes=64, tag="table_words")
        nc.sync.dma_start(table_words[:].bitcast(I32), tab_words[0].bitcast(I32))
        wor_rows = wor.rearrange("(p j) f -> p j f", j=PACK)
        wor_first = keep.tile([P, PACK, F // 2], F32, tag="wor_first")
        nc.sync.dma_start(wor_first[:], wor_rows[:, :, : F // 2])

        gain_sb = keep.tile([P, PACK], F32)
        nc.gpsimd.dma_start(gain_sb[:], gain.rearrange("(p t) o -> p (t o)", t=PACK))
        rs_sb = keep.tile([P, PACK], F32)
        nc.gpsimd.dma_start(rs_sb[:], rs.rearrange("(p t) o -> p (t o)", t=PACK))

        page = [keep.tile([P, U], F32, name=f"page{t}") for t in range(PACK)]
        for t in range(PACK):
            nc.vector.memset(page[t][:], 0.0)

        w1_dealt = [keep.tile([P, 2, P, PACK], BF16, name=f"w1_dealt{pair}", tag=f"w1_dealt{pair}", align_bytes=64) for pair in range(2)]
        for h in range(2):
            for pair, copy in enumerate((nc.vector.tensor_copy, nc.scalar.copy)):
                deal(copy, w1_dealt[pair][:, :, h * HALF : (h + 1) * HALF, :], by_place(w1_raw[h][:])[:, :, :, 2 * pair : 2 * pair + 2])

        ground_rows = ground.rearrange("(p t) u -> p t u", t=PACK)
        ground_early = keep.tile([P, EARLY_PLACES, U], F32, tag="w1_raw0")
        nc.sync.dma_start(ground_early[:], ground_rows[:, :EARLY_PLACES, :])
        wor_second = keep.tile([P, PACK, F // 2], F32, tag="w1_raw1")
        nc.sync.dma_start(wor_second[:], wor_rows[:, :, F // 2 :])
        wor_raw = (wor_first, wor_second)

        w1_first_codes = keep.tile([P, P], U32, align_bytes=64)
        w1_scales = keep.tile([P, PACK, P], U8, align_bytes=64)
        picked_scales = keep.tile([P, J], U8, align_bytes=64)
        picked_words = keep.tile([P, J], U16, align_bytes=64)

        def quantize_w1(t, codes):
            nc.vector.quantize_mx(
                out=codes.bitcast(FP8X4),
                scales=w1_scales[:, t, :],
                in_=w1_dealt[t // 2][:, t % 2, :, :].rearrange("p m j -> p (m j)"),
            )

        quantize_w1(0, w1_first_codes[:])
        nc.vector.tensor_copy(picked_scales[:], table_scales[:].indirect(offs_sb[:]))
        ground_late = keep.tile([P, PACK - EARLY_PLACES, U], F32, tag="table_scales")
        nc.sync.dma_start(ground_late[:], ground_rows[:, EARLY_PLACES:, :])
        nc.vector.tensor_copy(picked_words[:], table_words[:].indirect(offs_sb[:]))
        w1_later_codes = keep.tile([P, PACK - 1, P], U32, align_bytes=64, tag="table_words")
        w1_codes = [w1_first_codes[:]] + [w1_later_codes[:, t, :] for t in range(PACK - 1)]
        for t in range(1, PACK):
            quantize_w1(t, w1_codes[t])
        res_sb = keep.tile([P, PACK, U], F32, align_bytes=64, tag="w1_dealt0")
        nc.sync.dma_start(res_sb[:], res.rearrange("(p t) u -> p t u", t=PACK))

        h1 = [keep.tile([P, J], F32, name=f"h1_{t}") for t in range(PACK)]
        for t in range(PACK):
            a = psum.tile([P, J], F32, name=f"a{t}")
            nc.tensor.matmul_mx(
                out=a[:],
                lhsT=w1_codes[t].bitcast(FP8X4),
                lhsT_scale=w1_scales[:, t, :],
                rhs=picked_words[:].bitcast(FP4X4),
                rhs_scale=picked_scales[:],
                start=True,
                stop=True,
            )
            nc.scalar.activation(h1[t][:], a[:], COPY, scale=gain_sb[:, t : t + 1])

        ground_term = keep.tile([P, PACK, U], F32)
        wor_dealt = keep.tile([P, PACK, P, PACK], BF16, align_bytes=64, tag="table_words")
        wor_codes = keep.tile([P, PACK, P], U32, align_bytes=64)
        wor_scales = keep.tile([P, PACK, P], U8, align_bytes=64)

        ground_rs = [keep.tile([P, U], F32, name=f"ground_rs{t}") for t in range(EARLY_PLACES)]
        for t in range(EARLY_PLACES):
            nc.gpsimd.tensor_scalar(ground_rs[t][:], ground_early[:, t, :], rs_sb[:, t : t + 1], 0.0, MULT, ADD)

        def scatter(t):
            nc.vector.tensor_copy(page[t][:].indirect(offs2_sb[:]), h1[t][:])

        def deal_wor(piece):
            h, first = divmod(piece * WOR_PIECE, HALF)
            m0 = piece * WOR_PIECE
            deal(nc.scalar.copy, wor_dealt[:, :, m0 : m0 + WOR_PIECE, :], by_place(wor_raw[h][:, :, PACK * first : PACK * (first + WOR_PIECE)]))

        gate = []
        for t, tag in enumerate(("gate0", "wor_first")):
            scatter(t)
            deal_wor(t)
            early_gate = keep.tile([P, U], F32, name=f"gate{t}", tag=tag)
            gate.append(early_gate[:])
            nc.scalar.activation(gate[t], page[t][:], SIGMOID)
            nc.gpsimd.tensor_tensor(ground_term[:, t, :], gate[t], ground_rs[t][:], MULT)
        for piece in range(EARLY_PLACES, PACK):
            deal_wor(piece)

        late = keep.tile([P, 2 * PACK - EARLY_PLACES, U], F32, tag="w1_raw1")
        page_term = late[:, :PACK, :]
        gate.extend(late[:, PACK + i, :] for i in range(PACK - EARLY_PLACES))

        def page_term_on_scalar(t):
            nc.scalar.activation(page_term[:, t, :], page[t][:], COPY, scale=rs_sb[:, t : t + 1])

        def ground_term_on_vector(t):
            nc.vector.scalar_tensor_tensor(ground_term[:, t, :], gate[t], rs_sb[:, t : t + 1], ground_late[:, t - EARLY_PLACES, :], MULT, MULT)

        nc.vector.tensor_scalar(page_term[:, 0, :], page[0][:], rs_sb[:, 0:1], None, MULT)
        page_term_on_scalar(1)
        for t in range(EARLY_PLACES, PACK):
            scatter(t)
            nc.scalar.activation(gate[t], page[t][:], SIGMOID)
            page_term_on_scalar(t)
        ground_term_on_vector(PACK - 2)
        nc.vector.quantize_mx(
            out=wor_codes[:].rearrange("p t m -> p (t m)").bitcast(FP8X4),
            scales=wor_scales[:].rearrange("p t m -> p (t m)"),
            in_=wor_dealt[:].rearrange("p t m j -> p (t m j)"),
        )
        ground_term_on_vector(PACK - 1)

        fo1 = [keep.tile([P, PACK * CHUNK], BF16, name=f"fo1_{c}", align_bytes=64) for c in range(CHUNKS)]
        fo1_codes = [keep.tile([P, CHUNK], U32, name=f"fo1_codes{c}", align_bytes=64) for c in range(CHUNKS)]
        fo1_scales = [keep.tile([P, CHUNK], U8, name=f"fo1_scales{c}", align_bytes=64) for c in range(CHUNKS)]
        yo = [psum.tile([P, PACK, CHUNK], F32, name=f"yo{c}") for c in range(CHUNKS)]
        y = [keep.tile([P, PACK, CHUNK], F32, name=f"y{c}") for c in range(CHUNKS)]
        y_rounded = [keep.tile([P, PACK * CHUNK], BF16, name=f"y_rounded{c}", align_bytes=64) for c in range(CHUNKS)]
        y_codes = [keep.tile([P, 2 * CHUNK], U32, name=f"y_codes{g}", align_bytes=64) for g in range(CHUNKS // 2)]
        y_scales = keep.tile([P, U], U8, align_bytes=64)
        out_rows = out_0.rearrange("(p t) u -> p t u", t=PACK)
        out_words = out_1[0].rearrange("p c r -> p (c r)").bitcast(I32)

        def cols(c):
            return slice(c * CHUNK, (c + 1) * CHUNK)

        def add_terms(c):
            nc.vector.tensor_tensor(pairs_out(fo1[c][:]), pairs_in(page_term[:, :, cols(c)]), pairs_in(ground_term[:, :, cols(c)]), ADD)

        def last_layer(c):
            nc.vector.quantize_mx(out=fo1_codes[c][:].bitcast(FP8X4), scales=fo1_scales[c][:], in_=fo1[c][:])
            for t in range(PACK):
                nc.tensor.matmul_mx(
                    out=yo[c][:, t, :],
                    lhsT=wor_codes[:, t, :].bitcast(FP8X4),
                    lhsT_scale=wor_scales[:, t, :],
                    rhs=fo1_codes[c][:].bitcast(FP8X4),
                    rhs_scale=fo1_scales[c][:],
                    start=True,
                    stop=True,
                )

        def add_residual(c):
            nc.vector.tensor_tensor(y[c][:], yo[c][:], res_sb[:, :, cols(c)], ADD)
            nc.sync.dma_start(out_rows[:, :, cols(c)], y[c][:])
            nc.scalar.copy(pairs_out(y_rounded[c][:]), pairs_in(y[c][:]))

        def hand_on(c):
            g, second = divmod(c, 2)
            nc.vector.quantize_mx(out=y_codes[g][:, cols(second)].bitcast(FP8X4), scales=y_scales[:, cols(c)], in_=y_rounded[c][:])
            if second:
                nc.sync.dma_start(out_words[:, 2 * g * CHUNK : 2 * (g + 1) * CHUNK], y_codes[g][:].bitcast(I32))

        stages = ((add_terms, 0), (last_layer, 1), (add_residual, 3), (hand_on, 5))
        for step in range(CHUNKS + stages[-1][1]):
            for stage, lag in stages:
                if 0 <= step - lag < CHUNKS:
                    stage(step - lag)

        out_scale_rows = out_2[0].bitcast(I32).rearrange("(q i) c -> i q c", i=SCALE_ROWS)
        for i in range(SCALE_ROWS):
            queue = nc.scalar if i % 2 else nc.sync
            queue.dma_start(out_scale_rows[i], y_scales[i:P:QUADRANT, :].bitcast(I32))
